import numpy as np
import ml_dtypes


def mxq(x, axis, fmt="e4m3"):
    dtype, down = {"e4m3": (ml_dtypes.float8_e4m3fn, 7), "e5m2": (ml_dtypes.float8_e5m2, 14)}[fmt]
    v = np.moveaxis(np.asarray(x, np.float32).astype(ml_dtypes.bfloat16).astype(np.float64), axis, -1)
    blocks = v.reshape(v.shape[:-1] + (-1, 32))
    amax = np.abs(blocks).max(-1, keepdims=True)
    byte = np.maximum(np.where(amax > 0, np.frexp(amax)[1] - 1 + 127, 0) - down, 1)
    scale = np.exp2(byte - 127.0)
    codes = (blocks / scale).astype(np.float32).astype(dtype).astype(np.float64)
    return np.moveaxis((codes * scale).reshape(v.shape), -1, axis)


WIDE = False


def mx_kscale(k):
    if not WIDE:
        return np.ones(k)
    levels = np.array([10, -10, 5, -5, 0])
    if k % 512:
        return np.exp2(np.random.permutation(np.resize(levels, k // 32))).repeat(32)
    a = np.empty((k // 512, 16))
    for p in range(k // 512):
        a[p, :8] = np.random.permutation(np.resize(levels, 8))
        for g in range(8):
            far = levels[np.abs(levels - a[p, g]) >= 10]
            a[p, g + 8] = far[np.random.randint(len(far))]
    return np.exp2(a.ravel()).repeat(32)


def f64(x):
    return np.asarray(x).astype(np.float64)


def split(x):
    m, e = np.frexp(f64(x))
    hi = np.ldexp(np.trunc(16.0 * m) / 16.0, e)
    return hi, f64(x) - hi


def gelu(v):
    return 0.5 * v * (1.0 + np.tanh(np.sqrt(2.0 / np.pi) * (v + 0.044715 * v**3)))


K, M, T = 512, 1536, 1536


def setup_inputs():
    n = np.random.standard_normal
    s = mx_kscale(K)[:, None]
    return {
        "w": (n((K, M)) / np.sqrt(K) / s).astype(np.float32),
        "x": (n((K, T)) * s).astype(np.float32),
        "b": (0.3 * n(1536)).astype(np.float32),
    }


def reference(w, x, b):
    w_hi, w_lo = split(w)
    w_hi_, w_lo_ = mxq(w_hi, 0, "e4m3"), mxq(w_lo, 0, "e4m3")
    x_ = mxq(f64(x), 0, "e4m3")
    y = x_.T @ w_hi_ + x_.T @ w_lo_
    return gelu(y + f64(b)[None, :])

@@ -1,0 +1,200 @@
+from contextlib import ExitStack
+
+import concourse.mybir as mybir
+from concourse.masks import make_identity
+
+K, M, T = 512, 1536, 1536
+FLOPS = 2 * 2 * K * M * T
+
+F32 = mybir.dt.float32
+BF16 = mybir.dt.bfloat16
+U32 = mybir.dt.uint32
+I32 = mybir.dt.int32
+U8 = mybir.dt.uint8
+FP8X4 = mybir.dt.float8_e4m3fn_x4
+ALU = mybir.AluOpType
+ACT = mybir.ActivationFunctionType
+
+P = 128
+PACK = 4
+N = 512
+UNIT = 256
+HI_MASK = -1048576
+
+LOADS = [
+    ("w", 0, 256), ("w", 256, 256), ("x", 0, 256), ("x", 256, 256), ("x", 512, 512), ("x", 1024, 512), ("w", 512, 512), ("w", 1024, 512),
+]
+
+
+def tile_mix_hilo_tm_gelu_kernel(tc, w, x, b, out):
+    nc = tc.nc
+    with ExitStack() as ctx:
+        keep = ctx.enter_context(tc.tile_pool(name="keep", bufs=1))
+        psum = ctx.enter_context(tc.psum_pool(name="psum", bufs=8))
+        ctx.enter_context(tc.manual_schedule())
+
+        b_col = keep.tile([P, 12], F32, name="b_col")
+        nc.scalar.dma_start(out=b_col[:], in_=b.rearrange("(p m) -> p m", m=12))
+        raw = {}
+        for which, c0, width in LOADS:
+            t = keep.tile([P, PACK, width], F32, name="raw_%s%d" % (which, c0), align_bytes=64)
+            src = w if which == "w" else x
+            nc.sync.dma_start(out=t[:], in_=src[:, c0 : c0 + width].rearrange("(p j) c -> p j c", j=PACK))
+            raw[which, c0] = t
+
+        junk = keep.tile([P, 1], F32, name="junk")
+        nc.vector.memset(junk[:], 0.0)
+        nc.scalar.activation(out=junk[:], in_=junk[:], func=ACT.Gelu_apprx_tanh)
+        ident = keep.tile([P, P], F32, name="ident")
+        make_identity(nc, ident[:])
+
+        bias = keep.tile([P, M], F32, name="bias", align_bytes=64)
+        for k in range(3):
+            bank = psum.tile([P, N], F32, name="bank")
+            for m in range(4):
+                nc.tensor.transpose(bank[:, m * P : (m + 1) * P], b_col[:, 4 * k + m : 4 * k + m + 1].to_broadcast([P, P]), ident[:])
+            dst = bias[:].rearrange("q (p m) -> q p m", m=12)[:, :, 4 * k : 4 * k + 4]
+            src = bank[:].rearrange("q (m p) -> q p m", m=4)
+            if k == 1:
+                nc.scalar.copy(out=dst, in_=src)
+            else:
+                nc.vector.tensor_copy(out=dst, in_=src)
+
+        hi32, hib, lob, hic, his, loc, los = {}, {}, {}, {}, {}, {}, {}
+        for g in range(3):
+            hi32[g] = keep.tile([P, PACK, N], F32, name="hi32_%d" % g, align_bytes=64)
+            hib[g] = keep.tile([P, N, PACK], BF16, name="hib_%d" % g, align_bytes=64)
+            lob[g] = keep.tile([P, N, PACK], BF16, name="lob_%d" % g, align_bytes=64)
+            hic[g] = keep.tile([P, N], U32, name="hic_%d" % g, align_bytes=64)
+            loc[g] = keep.tile([P, N], U32, name="loc_%d" % g, align_bytes=64)
+            his[g] = keep.tile([P, N], U8, name="his_%d" % g, align_bytes=64)
+            los[g] = keep.tile([P, N], U8, name="los_%d" % g, align_bytes=64)
+        xb = keep.tile([P, T, PACK], BF16, name="xb", align_bytes=64)
+        xcodes = keep.tile([P, T], U32, name="xcodes", align_bytes=64)
+        xscales = keep.tile([P, T], U8, name="xscales", align_bytes=64)
+
+        def raw_part(which, c0, width):
+            for (wh, r0), t in raw.items():
+                if wh == which and r0 <= c0 and c0 + width <= r0 + t.shape[2]:
+                    return t[:, :, c0 - r0 : c0 - r0 + width]
+            raise ValueError("no such columns")
+
+        def read4(v):
+            return v.rearrange("p t (c i) -> p c t i", i=4)
+
+        def write4(v):
+            return v.rearrange("p (c i) t -> p c t i", i=4)
+
+        def mask(c0, width):
+            g, o = c0 // N, c0 % N
+            nc.vector.tensor_scalar(
+                out=hi32[g][:, :, o : o + width].bitcast(I32), in0=raw_part("w", c0, width).bitcast(I32),
+                scalar1=HI_MASK, scalar2=None, op0=ALU.bitwise_and)
+
+        def hicast(c0, width):
+            g, o = c0 // N, c0 % N
+            nc.scalar.copy(out=write4(hib[g][:, o : o + width, :]), in_=read4(hi32[g][:, :, o : o + width]))
+
+        def sub(eng, c0, width):
+            g, o = c0 // N, c0 % N
+            eng.tensor_tensor(
+                out=write4(lob[g][:, o : o + width, :]), in0=read4(raw_part("w", c0, width)),
+                in1=read4(hi32[g][:, :, o : o + width]), op=ALU.subtract)
+
+        def hicast_g(c0, width):
+            g, o = c0 // N, c0 % N
+            nc.gpsimd.tensor_scalar(
+                out=write4(hib[g][:, o : o + width, :]), in0=read4(hi32[g][:, :, o : o + width]),
+                scalar1=1.0, scalar2=0.0, op0=ALU.mult, op1=ALU.add)
+
+        def xcast_v(c0, width):
+            nc.vector.tensor_copy(out=write4(xb[:, c0 : c0 + width, :]), in_=read4(raw_part("x", c0, width)))
+
+        def qhi(g):
+            nc.vector.quantize_mx(out=hic[g][:].bitcast(FP8X4), scales=his[g][:], in_=hib[g][:].rearrange("p c t -> p (c t)"))
+
+        def qlo(g):
+            nc.vector.quantize_mx(out=loc[g][:].bitcast(FP8X4), scales=los[g][:], in_=lob[g][:].rearrange("p c t -> p (c t)"))
+
+        def xcast_s(c0, width):
+            nc.scalar.copy(out=write4(xb[:, c0 : c0 + width, :]), in_=read4(raw_part("x", c0, width)))
+
+        def xcast_g(c0, width):
+            nc.gpsimd.tensor_scalar(
+                out=write4(xb[:, c0 : c0 + width, :]), in0=read4(raw_part("x", c0, width)),
+                scalar1=1.0, scalar2=0.0, op0=ALU.mult, op1=ALU.add)
+
+        def qx(c0, width):
+            nc.vector.quantize_mx(
+                out=xcodes[:, c0 : c0 + width].bitcast(FP8X4), scales=xscales[:, c0 : c0 + width],
+                in_=xb[:, c0 : c0 + width, :].rearrange("p c t -> p (c t)"))
+
+        res = {}
+        for t in range(12):
+            res[t] = keep.tile([P, M], F32, name="res_%d" % t, align_bytes=64)
+        acc = {}
+
+        def mm(t, g):
+            bank = psum.tile([P, N], F32, name="bank")
+            acc[t, g] = bank
+            for i, (codes, scales) in enumerate(((hic, his), (loc, los))):
+                nc.tensor.matmul_mx(
+                    out=bank[:], lhsT=xcodes[:, t * P : (t + 1) * P].bitcast(FP8X4), lhsT_scale=xscales[:, t * P : (t + 1) * P],
+                    rhs=codes[g][:].bitcast(FP8X4), rhs_scale=scales[g][:], start=(i == 0), stop=(i == 1))
+
+        def add(t, g):
+            nc.vector.tensor_tensor(out=res[t][:, g * N : (g + 1) * N], in0=acc[t, g][:], in1=bias[:, g * N : (g + 1) * N], op=ALU.add)
+
+        def gelu(t, c0, width):
+            nc.scalar.activation(out=res[t][:, c0 : c0 + width], in_=res[t][:, c0 : c0 + width], func=ACT.Gelu_apprx_tanh)
+
+        def store(t, c0, width):
+            nc.sync.dma_start(out=out[t * P : (t + 1) * P, c0 : c0 + width], in_=res[t][:, c0 : c0 + width])
+
+        def block(ts, g):
+            for t in ts:
+                mm(t, g)
+                add(t, g)
+                gelu(t, g * N, N)
+                store(t, g * N, N)
+
+        mask(0, 256)
+        hicast(0, 256)
+        mask(256, 256)
+        hicast(256, 256)
+        sub(nc.vector, 0, 256)
+        sub(nc.vector, 256, 256)
+        xcast_s(0, 256)
+        xcast_s(256, 256)
+        qhi(0)
+        qlo(0)
+        qx(0, 256)
+        qx(256, 256)
+        xcast_s(512, 256)
+        xcast_v(768, 256)
+        xcast_s(1024, 256)
+        xcast_g(1280, 256)
+        block(range(0, 2), 0)
+        qx(512, 512)
+        block(range(2, 5), 0)
+        qx(1024, 512)
+        mask(512, 512)
+        sub(nc.gpsimd, 512, 256)
+        sub(nc.gpsimd, 768, 256)
+        block(range(5, 7), 0)
+        hicast(512, 256)
+        block(range(7, 9), 0)
+        hicast(768, 256)
+        block(range(9, 12), 0)
+        qhi(1)
+        qlo(1)
+        mask(1024, 512)
+        hicast_g(1024, 256)
+        hicast(1280, 256)
+        sub(nc.gpsimd, 1024, 256)
+        sub(nc.gpsimd, 1280, 256)
+        block(range(0, 10), 1)
+        qhi(2)
+        qlo(2)
+        block(range(10, 12), 1)
+        block(range(0, 12), 2)

@@ -22,7 +22,7 @@ UNIT = 256
 HI_MASK = -1048576
 
 LOADS = [
-    ("w", 0, 256), ("w", 256, 256), ("x", 0, 256), ("x", 256, 256), ("x", 512, 512), ("x", 1024, 512), ("w", 512, 512), ("w", 1024, 512),
+    ("w", 0, 256), ("w", 256, 256), ("x", 512, 512), ("w", 512, 512), ("x", 256, 256), ("x", 0, 256), ("x", 1024, 512), ("w", 1024, 512),
 ]
 
 
@@ -110,6 +110,10 @@ def tile_mix_hilo_tm_gelu_kernel(tc, w, x, b, out):
         def xcast_v(c0, width):
             nc.vector.tensor_copy(out=write4(xb[:, c0 : c0 + width, :]), in_=read4(raw_part("x", c0, width)))
 
+        def hicast_v(c0, width):
+            g, o = c0 // N, c0 % N
+            nc.vector.tensor_copy(out=write4(hib[g][:, o : o + width, :]), in_=read4(hi32[g][:, :, o : o + width]))
+
         def qhi(g):
             nc.vector.quantize_mx(out=hic[g][:].bitcast(FP8X4), scales=his[g][:], in_=hib[g][:].rearrange("p c t -> p (c t)"))
 
@@ -145,56 +149,192 @@ def tile_mix_hilo_tm_gelu_kernel(tc, w, x, b, out):
         def add(t, g):
             nc.vector.tensor_tensor(out=res[t][:, g * N : (g + 1) * N], in0=acc[t, g][:], in1=bias[:, g * N : (g + 1) * N], op=ALU.add)
 
+        def cp(t, g):
+            nc.scalar.copy(out=res[t][:, g * N : (g + 1) * N], in_=acc[t, g][:])
+
+        def addg(t, g):
+            nc.gpsimd.tensor_tensor(out=res[t][:, g * N : (g + 1) * N], in0=res[t][:, g * N : (g + 1) * N], in1=bias[:, g * N : (g + 1) * N], op=ALU.add)
+
         def gelu(t, c0, width):
             nc.scalar.activation(out=res[t][:, c0 : c0 + width], in_=res[t][:, c0 : c0 + width], func=ACT.Gelu_apprx_tanh)
 
         def store(t, c0, width):
             nc.sync.dma_start(out=out[t * P : (t + 1) * P, c0 : c0 + width], in_=res[t][:, c0 : c0 + width])
 
-        def block(ts, g):
-            for t in ts:
-                mm(t, g)
-                add(t, g)
-                gelu(t, g * N, N)
-                store(t, g * N, N)
-
         mask(0, 256)
-        hicast(0, 256)
         mask(256, 256)
         hicast(256, 256)
-        sub(nc.vector, 0, 256)
         sub(nc.vector, 256, 256)
-        xcast_s(0, 256)
+        hicast(0, 256)
+        xcast_s(768, 256)
+        xcast_s(512, 256)
+        sub(nc.vector, 0, 256)
+        qlo(0)
         xcast_s(256, 256)
         qhi(0)
-        qlo(0)
-        qx(0, 256)
-        qx(256, 256)
-        xcast_s(512, 256)
-        xcast_v(768, 256)
-        xcast_s(1024, 256)
-        xcast_g(1280, 256)
-        block(range(0, 2), 0)
-        qx(512, 512)
-        block(range(2, 5), 0)
-        qx(1024, 512)
         mask(512, 512)
-        sub(nc.gpsimd, 512, 256)
-        sub(nc.gpsimd, 768, 256)
-        block(range(5, 7), 0)
-        hicast(512, 256)
-        block(range(7, 9), 0)
         hicast(768, 256)
-        block(range(9, 12), 0)
+        qx(512, 512)
+        sub(nc.vector, 512, 256)
+        mm(7, 0)
+        qx(256, 256)
+        mm(5, 0)
+        hicast(512, 256)
+        add(7, 0)
+        mm(2, 0)
+        mm(4, 0)
+        sub(nc.gpsimd, 768, 256)
+        mm(6, 0)
+        xcast_s(0, 256)
+        add(5, 0)
+        mm(3, 0)
+        add(2, 0)
+        xcast_s(1280, 256)
+        add(4, 0)
+        add(6, 0)
         qhi(1)
         qlo(1)
+        mm(5, 1)
+        qx(0, 256)
         mask(1024, 512)
-        hicast_g(1024, 256)
-        hicast(1280, 256)
-        sub(nc.gpsimd, 1024, 256)
+        xcast_s(1024, 256)
+        qx(1024, 512)
+        mm(0, 0)
+        mm(4, 1)
+        mm(1, 1)
+        gelu(2, 0 * N, 1 * N)
+        store(2, 0 * N, 1 * N)
+        add(5, 1)
+        mm(8, 1)
+        gelu(4, 0 * N, 1 * N)
+        store(4, 0 * N, 1 * N)
+        gelu(5, 0 * N, 1 * N)
+        store(5, 0 * N, 1 * N)
+        add(0, 0)
+        gelu(6, 0 * N, 1 * N)
+        store(6, 0 * N, 1 * N)
+        add(3, 0)
+        mm(11, 0)
+        mm(10, 1)
+        gelu(0, 0 * N, 1 * N)
+        store(0, 0 * N, 1 * N)
+        mm(0, 1)
         sub(nc.gpsimd, 1280, 256)
-        block(range(0, 10), 1)
-        qhi(2)
+        gelu(7, 0 * N, 1 * N)
+        store(7, 0 * N, 1 * N)
+        add(8, 1)
+        gelu(3, 0 * N, 1 * N)
+        store(3, 0 * N, 1 * N)
+        add(4, 1)
+        mm(10, 0)
+        hicast_g(1024, 256)
+        gelu(4, 1 * N, 1 * N)
+        store(4, 1 * N, 1 * N)
+        add(10, 1)
+        mm(1, 0)
+        add(1, 1)
+        add(11, 0)
+        gelu(8, 1 * N, 1 * N)
+        store(8, 1 * N, 1 * N)
+        mm(6, 1)
+        mm(2, 1)
+        add(0, 1)
+        mm(7, 1)
+        gelu(5, 1 * N, 1 * N)
+        store(5, 1 * N, 1 * N)
+        add(1, 0)
+        gelu(10, 1 * N, 1 * N)
+        store(10, 1 * N, 1 * N)
+        add(10, 0)
+        gelu(11, 0 * N, 1 * N)
+        store(11, 0 * N, 1 * N)
+        gelu(1, 0 * N, 1 * N)
+        store(1, 0 * N, 1 * N)
+        add(2, 1)
+        sub(nc.gpsimd, 1024, 256)
+        gelu(0, 1 * N, 1 * N)
+        store(0, 1 * N, 1 * N)
+        add(6, 1)
+        mm(9, 0)
+        gelu(1, 1 * N, 1 * N)
+        store(1, 1 * N, 1 * N)
+        add(7, 1)
+        mm(11, 1)
+        mm(3, 1)
+        hicast_v(1280, 256)
+        gelu(6, 1 * N, 1 * N)
+        store(6, 1 * N, 1 * N)
         qlo(2)
-        block(range(10, 12), 1)
-        block(range(0, 12), 2)
+        mm(9, 1)
+        gelu(7, 1 * N, 1 * N)
+        store(7, 1 * N, 1 * N)
+        mm(8, 0)
+        qhi(2)
+        mm(0, 2)
+        cp(3, 1)
+        gelu(2, 1 * N, 1 * N)
+        store(2, 1 * N, 1 * N)
+        add(9, 0)
+        gelu(10, 0 * N, 1 * N)
+        store(10, 0 * N, 1 * N)
+        mm(11, 2)
+        gelu(9, 0 * N, 1 * N)
+        store(9, 0 * N, 1 * N)
+        add(9, 1)
+        add(8, 0)
+        add(11, 1)
+        gelu(9, 1 * N, 1 * N)
+        store(9, 1 * N, 1 * N)
+        mm(4, 2)
+        add(0, 2)
+        mm(10, 2)
+        addg(3, 1)
+        gelu(3, 1 * N, 1 * N)
+        store(3, 1 * N, 1 * N)
+        gelu(11, 1 * N, 1 * N)
+        store(11, 1 * N, 1 * N)
+        gelu(8, 0 * N, 1 * N)
+        store(8, 0 * N, 1 * N)
+        add(11, 2)
+        mm(7, 2)
+        mm(2, 2)
+        gelu(11, 2 * N, 1 * N)
+        store(11, 2 * N, 1 * N)
+        mm(9, 2)
+        mm(1, 2)
+        add(10, 2)
+        add(7, 2)
+        gelu(0, 2 * N, 1 * N)
+        store(0, 2 * N, 1 * N)
+        mm(8, 2)
+        add(4, 2)
+        gelu(10, 2 * N, 1 * N)
+        store(10, 2 * N, 1 * N)
+        add(8, 2)
+        add(9, 2)
+        mm(3, 2)
+        mm(5, 2)
+        add(2, 2)
+        mm(6, 2)
+        gelu(7, 2 * N, 1 * N)
+        store(7, 2 * N, 1 * N)
+        gelu(4, 2 * N, 1 * N)
+        store(4, 2 * N, 1 * N)
+        add(1, 2)
+        gelu(8, 2 * N, 1 * N)
+        store(8, 2 * N, 1 * N)
+        gelu(9, 2 * N, 1 * N)
+        store(9, 2 * N, 1 * N)
+        gelu(2, 2 * N, 1 * N)
+        store(2, 2 * N, 1 * N)
+        gelu(1, 2 * N, 1 * N)
+        store(1, 2 * N, 1 * N)
+        add(3, 2)
+        add(5, 2)
+        gelu(5, 2 * N, 1 * N)
+        store(5, 2 * N, 1 * N)
+        add(6, 2)
+        gelu(6, 2 * N, 1 * N)
+        store(6, 2 * N, 1 * N)
+        gelu(3, 2 * N, 1 * N)
+        store(3, 2 * N, 1 * N)

from contextlib import ExitStack

import concourse.mybir as mybir
from concourse.masks import make_identity

K, M, T = 512, 1536, 1536
FLOPS = 2 * 2 * K * M * T

F32 = mybir.dt.float32
BF16 = mybir.dt.bfloat16
U32 = mybir.dt.uint32
I32 = mybir.dt.int32
U8 = mybir.dt.uint8
FP8X4 = mybir.dt.float8_e4m3fn_x4
ALU = mybir.AluOpType
ACT = mybir.ActivationFunctionType

P = 128
PACK = 4
N = 512
UNIT = 256
HI_MASK = -1048576

LOADS = [
    ("w", 0, 256), ("w", 256, 256), ("x", 512, 512), ("w", 512, 512), ("x", 256, 256), ("x", 0, 256), ("x", 1024, 512), ("w", 1024, 512),
]


def tile_mix_hilo_tm_gelu_kernel(tc, w, x, b, out):
    nc = tc.nc
    with ExitStack() as ctx:
        keep = ctx.enter_context(tc.tile_pool(name="keep", bufs=1))
        psum = ctx.enter_context(tc.psum_pool(name="psum", bufs=8))
        ctx.enter_context(tc.manual_schedule())

        b_col = keep.tile([P, 12], F32, name="b_col")
        nc.scalar.dma_start(out=b_col[:], in_=b.rearrange("(p m) -> p m", m=12))
        raw = {}
        for which, c0, width in LOADS:
            t = keep.tile([P, PACK, width], F32, name="raw_%s%d" % (which, c0), align_bytes=64)
            src = w if which == "w" else x
            nc.sync.dma_start(out=t[:], in_=src[:, c0 : c0 + width].rearrange("(p j) c -> p j c", j=PACK))
            raw[which, c0] = t

        junk = keep.tile([P, 1], F32, name="junk")
        nc.vector.memset(junk[:], 0.0)
        nc.scalar.activation(out=junk[:], in_=junk[:], func=ACT.Gelu_apprx_tanh)
        ident = keep.tile([P, P], F32, name="ident")
        make_identity(nc, ident[:])

        bias = keep.tile([P, M], F32, name="bias", align_bytes=64)
        for k in range(3):
            bank = psum.tile([P, N], F32, name="bank")
            for m in range(4):
                nc.tensor.transpose(bank[:, m * P : (m + 1) * P], b_col[:, 4 * k + m : 4 * k + m + 1].to_broadcast([P, P]), ident[:])
            dst = bias[:].rearrange("q (p m) -> q p m", m=12)[:, :, 4 * k : 4 * k + 4]
            src = bank[:].rearrange("q (m p) -> q p m", m=4)
            if k == 1:
                nc.scalar.copy(out=dst, in_=src)
            else:
                nc.vector.tensor_copy(out=dst, in_=src)

        hi32, hib, lob, hic, his, loc, los = {}, {}, {}, {}, {}, {}, {}
        for g in range(3):
            hi32[g] = keep.tile([P, PACK, N], F32, name="hi32_%d" % g, align_bytes=64)
            hib[g] = keep.tile([P, N, PACK], BF16, name="hib_%d" % g, align_bytes=64)
            lob[g] = keep.tile([P, N, PACK], BF16, name="lob_%d" % g, align_bytes=64)
            hic[g] = keep.tile([P, N], U32, name="hic_%d" % g, align_bytes=64)
            loc[g] = keep.tile([P, N], U32, name="loc_%d" % g, align_bytes=64)
            his[g] = keep.tile([P, N], U8, name="his_%d" % g, align_bytes=64)
            los[g] = keep.tile([P, N], U8, name="los_%d" % g, align_bytes=64)
        xb = keep.tile([P, T, PACK], BF16, name="xb", align_bytes=64)
        xcodes = keep.tile([P, T], U32, name="xcodes", align_bytes=64)
        xscales = keep.tile([P, T], U8, name="xscales", align_bytes=64)

        def raw_part(which, c0, width):
            for (wh, r0), t in raw.items():
                if wh == which and r0 <= c0 and c0 + width <= r0 + t.shape[2]:
                    return t[:, :, c0 - r0 : c0 - r0 + width]
            raise ValueError("no such columns")

        def read4(v):
            return v.rearrange("p t (c i) -> p c t i", i=4)

        def write4(v):
            return v.rearrange("p (c i) t -> p c t i", i=4)

        def mask(c0, width):
            g, o = c0 // N, c0 % N
            nc.vector.tensor_scalar(
                out=hi32[g][:, :, o : o + width].bitcast(I32), in0=raw_part("w", c0, width).bitcast(I32),
                scalar1=HI_MASK, scalar2=None, op0=ALU.bitwise_and)

        def hicast(c0, width):
            g, o = c0 // N, c0 % N
            nc.scalar.copy(out=write4(hib[g][:, o : o + width, :]), in_=read4(hi32[g][:, :, o : o + width]))

        def sub(eng, c0, width):
            g, o = c0 // N, c0 % N
            eng.tensor_tensor(
                out=write4(lob[g][:, o : o + width, :]), in0=read4(raw_part("w", c0, width)),
                in1=read4(hi32[g][:, :, o : o + width]), op=ALU.subtract)

        def hicast_g(c0, width):
            g, o = c0 // N, c0 % N
            nc.gpsimd.tensor_scalar(
                out=write4(hib[g][:, o : o + width, :]), in0=read4(hi32[g][:, :, o : o + width]),
                scalar1=1.0, scalar2=0.0, op0=ALU.mult, op1=ALU.add)

        def xcast_v(c0, width):
            nc.vector.tensor_copy(out=write4(xb[:, c0 : c0 + width, :]), in_=read4(raw_part("x", c0, width)))

        def hicast_v(c0, width):
            g, o = c0 // N, c0 % N
            nc.vector.tensor_copy(out=write4(hib[g][:, o : o + width, :]), in_=read4(hi32[g][:, :, o : o + width]))

        def qhi(g):
            nc.vector.quantize_mx(out=hic[g][:].bitcast(FP8X4), scales=his[g][:], in_=hib[g][:].rearrange("p c t -> p (c t)"))

        def qlo(g):
            nc.vector.quantize_mx(out=loc[g][:].bitcast(FP8X4), scales=los[g][:], in_=lob[g][:].rearrange("p c t -> p (c t)"))

        def xcast_s(c0, width):
            nc.scalar.copy(out=write4(xb[:, c0 : c0 + width, :]), in_=read4(raw_part("x", c0, width)))

        def xcast_g(c0, width):
            nc.gpsimd.tensor_scalar(
                out=write4(xb[:, c0 : c0 + width, :]), in0=read4(raw_part("x", c0, width)),
                scalar1=1.0, scalar2=0.0, op0=ALU.mult, op1=ALU.add)

        def qx(c0, width):
            nc.vector.quantize_mx(
                out=xcodes[:, c0 : c0 + width].bitcast(FP8X4), scales=xscales[:, c0 : c0 + width],
                in_=xb[:, c0 : c0 + width, :].rearrange("p c t -> p (c t)"))

        res = {}
        for t in range(12):
            res[t] = keep.tile([P, M], F32, name="res_%d" % t, align_bytes=64)
        acc = {}

        def mm(t, g):
            bank = psum.tile([P, N], F32, name="bank")
            acc[t, g] = bank
            for i, (codes, scales) in enumerate(((hic, his), (loc, los))):
                nc.tensor.matmul_mx(
                    out=bank[:], lhsT=xcodes[:, t * P : (t + 1) * P].bitcast(FP8X4), lhsT_scale=xscales[:, t * P : (t + 1) * P],
                    rhs=codes[g][:].bitcast(FP8X4), rhs_scale=scales[g][:], start=(i == 0), stop=(i == 1))

        def add(t, g):
            nc.vector.tensor_tensor(out=res[t][:, g * N : (g + 1) * N], in0=acc[t, g][:], in1=bias[:, g * N : (g + 1) * N], op=ALU.add)

        def cp(t, g):
            nc.scalar.copy(out=res[t][:, g * N : (g + 1) * N], in_=acc[t, g][:])

        def addg(t, g):
            nc.gpsimd.tensor_tensor(out=res[t][:, g * N : (g + 1) * N], in0=res[t][:, g * N : (g + 1) * N], in1=bias[:, g * N : (g + 1) * N], op=ALU.add)

        def gelu(t, c0, width):
            nc.scalar.activation(out=res[t][:, c0 : c0 + width], in_=res[t][:, c0 : c0 + width], func=ACT.Gelu_apprx_tanh)

        def store(t, c0, width):
            nc.sync.dma_start(out=out[t * P : (t + 1) * P, c0 : c0 + width], in_=res[t][:, c0 : c0 + width])

        mask(0, 256)
        mask(256, 256)
        hicast(256, 256)
        sub(nc.vector, 256, 256)
        hicast(0, 256)
        xcast_s(768, 256)
        xcast_s(512, 256)
        sub(nc.vector, 0, 256)
        qlo(0)
        xcast_s(256, 256)
        qhi(0)
        mask(512, 512)
        hicast(768, 256)
        qx(512, 512)
        sub(nc.vector, 512, 256)
        mm(7, 0)
        qx(256, 256)
        mm(5, 0)
        hicast(512, 256)
        add(7, 0)
        mm(2, 0)
        mm(4, 0)
        sub(nc.gpsimd, 768, 256)
        mm(6, 0)
        xcast_s(0, 256)
        add(5, 0)
        mm(3, 0)
        add(2, 0)
        xcast_s(1280, 256)
        add(4, 0)
        add(6, 0)
        qhi(1)
        qlo(1)
        mm(5, 1)
        qx(0, 256)
        mask(1024, 512)
        xcast_s(1024, 256)
        qx(1024, 512)
        mm(0, 0)
        mm(4, 1)
        mm(1, 1)
        gelu(2, 0 * N, 1 * N)
        store(2, 0 * N, 1 * N)
        add(5, 1)
        mm(8, 1)
        gelu(4, 0 * N, 1 * N)
        store(4, 0 * N, 1 * N)
        gelu(5, 0 * N, 1 * N)
        store(5, 0 * N, 1 * N)
        add(0, 0)
        gelu(6, 0 * N, 1 * N)
        store(6, 0 * N, 1 * N)
        add(3, 0)
        mm(11, 0)
        mm(10, 1)
        gelu(0, 0 * N, 1 * N)
        store(0, 0 * N, 1 * N)
        mm(0, 1)
        sub(nc.gpsimd, 1280, 256)
        gelu(7, 0 * N, 1 * N)
        store(7, 0 * N, 1 * N)
        add(8, 1)
        gelu(3, 0 * N, 1 * N)
        store(3, 0 * N, 1 * N)
        add(4, 1)
        mm(10, 0)
        hicast_g(1024, 256)
        gelu(4, 1 * N, 1 * N)
        store(4, 1 * N, 1 * N)
        add(10, 1)
        mm(1, 0)
        add(1, 1)
        add(11, 0)
        gelu(8, 1 * N, 1 * N)
        store(8, 1 * N, 1 * N)
        mm(6, 1)
        mm(2, 1)
        add(0, 1)
        mm(7, 1)
        gelu(5, 1 * N, 1 * N)
        store(5, 1 * N, 1 * N)
        add(1, 0)
        gelu(10, 1 * N, 1 * N)
        store(10, 1 * N, 1 * N)
        add(10, 0)
        gelu(11, 0 * N, 1 * N)
        store(11, 0 * N, 1 * N)
        gelu(1, 0 * N, 1 * N)
        store(1, 0 * N, 1 * N)
        add(2, 1)
        sub(nc.gpsimd, 1024, 256)
        gelu(0, 1 * N, 1 * N)
        store(0, 1 * N, 1 * N)
        add(6, 1)
        mm(9, 0)
        gelu(1, 1 * N, 1 * N)
        store(1, 1 * N, 1 * N)
        add(7, 1)
        mm(11, 1)
        mm(3, 1)
        hicast_v(1280, 256)
        gelu(6, 1 * N, 1 * N)
        store(6, 1 * N, 1 * N)
        qlo(2)
        mm(9, 1)
        gelu(7, 1 * N, 1 * N)
        store(7, 1 * N, 1 * N)
        mm(8, 0)
        qhi(2)
        mm(0, 2)
        cp(3, 1)
        gelu(2, 1 * N, 1 * N)
        store(2, 1 * N, 1 * N)
        add(9, 0)
        gelu(10, 0 * N, 1 * N)
        store(10, 0 * N, 1 * N)
        mm(11, 2)
        gelu(9, 0 * N, 1 * N)
        store(9, 0 * N, 1 * N)
        add(9, 1)
        add(8, 0)
        add(11, 1)
        gelu(9, 1 * N, 1 * N)
        store(9, 1 * N, 1 * N)
        mm(4, 2)
        add(0, 2)
        mm(10, 2)
        addg(3, 1)
        gelu(3, 1 * N, 1 * N)
        store(3, 1 * N, 1 * N)
        gelu(11, 1 * N, 1 * N)
        store(11, 1 * N, 1 * N)
        gelu(8, 0 * N, 1 * N)
        store(8, 0 * N, 1 * N)
        add(11, 2)
        mm(7, 2)
        mm(2, 2)
        gelu(11, 2 * N, 1 * N)
        store(11, 2 * N, 1 * N)
        mm(9, 2)
        mm(1, 2)
        add(10, 2)
        add(7, 2)
        gelu(0, 2 * N, 1 * N)
        store(0, 2 * N, 1 * N)
        mm(8, 2)
        add(4, 2)
        gelu(10, 2 * N, 1 * N)
        store(10, 2 * N, 1 * N)
        add(8, 2)
        add(9, 2)
        mm(3, 2)
        mm(5, 2)
        add(2, 2)
        mm(6, 2)
        gelu(7, 2 * N, 1 * N)
        store(7, 2 * N, 1 * N)
        gelu(4, 2 * N, 1 * N)
        store(4, 2 * N, 1 * N)
        add(1, 2)
        gelu(8, 2 * N, 1 * N)
        store(8, 2 * N, 1 * N)
        gelu(9, 2 * N, 1 * N)
        store(9, 2 * N, 1 * N)
        gelu(2, 2 * N, 1 * N)
        store(2, 2 * N, 1 * N)
        gelu(1, 2 * N, 1 * N)
        store(1, 2 * N, 1 * N)
        add(3, 2)
        add(5, 2)
        gelu(5, 2 * N, 1 * N)
        store(5, 2 * N, 1 * N)
        add(6, 2)
        gelu(6, 2 * N, 1 * N)
        store(6, 2 * N, 1 * N)
        gelu(3, 2 * N, 1 * N)
        store(3, 2 * N, 1 * N)
